import numpy as np
import ml_dtypes


def mxq(x, axis, fmt="e4m3"):
    dtype, down = {"e4m3": (ml_dtypes.float8_e4m3fn, 7), "e5m2": (ml_dtypes.float8_e5m2, 14)}[fmt]
    v = np.moveaxis(np.asarray(x, np.float32).astype(ml_dtypes.bfloat16).astype(np.float64), axis, -1)
    blocks = v.reshape(v.shape[:-1] + (-1, 32))
    amax = np.abs(blocks).max(-1, keepdims=True)
    byte = np.maximum(np.where(amax > 0, np.frexp(amax)[1] - 1 + 127, 0) - down, 1)
    scale = np.exp2(byte - 127.0)
    codes = (blocks / scale).astype(np.float32).astype(dtype).astype(np.float64)
    return np.moveaxis((codes * scale).reshape(v.shape), -1, axis)


WIDE = False


def mx_kscale(k):
    if not WIDE:
        return np.ones(k)
    levels = np.array([10, -10, 5, -5, 0])
    if k % 512:
        return np.exp2(np.random.permutation(np.resize(levels, k // 32))).repeat(32)
    a = np.empty((k // 512, 16))
    for p in range(k // 512):
        a[p, :8] = np.random.permutation(np.resize(levels, 8))
        for g in range(8):
            far = levels[np.abs(levels - a[p, g]) >= 10]
            a[p, g + 8] = far[np.random.randint(len(far))]
    return np.exp2(a.ravel()).repeat(32)


def f64(x):
    return np.asarray(x).astype(np.float64)


def striped(idx):
    return np.tile(np.asarray(idx).reshape(-1, 16).T, (8, 1)).astype(np.uint16)


def unstriped(offs):
    return offs[:16].T.reshape(-1).astype(np.int64)


E2M1 = np.array([0.0, 0.5, 1.0, 1.5, 2.0, 3.0, 4.0, 6.0, -0.0, -0.5, -1.0, -1.5, -2.0, -3.0, -4.0, -6.0])


def pack_weight(w, fmt):
    k, n = w.shape
    w = f64(np.asarray(w, np.float32).astype(ml_dtypes.bfloat16)).reshape(k // 32, 32, n)
    amax = np.abs(w).max(1)
    if fmt == "e4m3":
        byte = np.frexp(amax)[1] - 1 + 127 - 7
    else:
        mant, ex = np.frexp(amax / 6.0)
        byte = np.where(mant > 0.5, ex, ex - 1) + 127
    byte = np.clip(np.where(amax > 0, byte, 1), 1, 254)
    scaled = (w * np.exp2(127.0 - byte)[:, None, :]).reshape(k, n).astype(np.float32)
    by_word = np.ascontiguousarray(scaled.reshape(k // 512, 128, 4, n).transpose(0, 1, 3, 2))
    if fmt == "e4m3":
        words = by_word.astype(ml_dtypes.float8_e4m3fn).view(np.uint8)
    else:
        c = by_word.astype(ml_dtypes.float4_e2m1fn).view(np.uint8) & 0xF
        words = (c[..., 0::2] | (c[..., 1::2] << 4)).reshape(k // 512, 128, 2 * n)
    return np.ascontiguousarray(words), np.ascontiguousarray(byte.astype(np.uint8).reshape(k // 512, 16, n))


def unpack_weight(words, scales, fmt):
    g, _, n = scales.shape
    words = np.ascontiguousarray(words).reshape(g, 128, n, -1)
    if fmt == "e4m3":
        vals = words.view(ml_dtypes.float8_e4m3fn).astype(np.float64)
    else:
        nib = np.empty((g, 128, n, 4), np.uint8)
        nib[..., 0::2] = words & 0xF
        nib[..., 1::2] = words >> 4
        vals = E2M1[nib]
    vals = vals * np.repeat(np.exp2(scales.astype(np.float64) - 127.0), 8, axis=1)[..., None]
    return vals.transpose(0, 1, 3, 2).reshape(g * 512, n)


B, N, T, D, NQ = 1, 512, 2048, 1024, 512
DV = 512


def sgn(shape):
    return np.random.uniform(0.5, 2.0, shape) * np.where(np.random.standard_normal(shape) < 0, -1.0, 1.0)


def setup_inputs():
    n = np.random.standard_normal
    idx = np.random.permutation(T)[:B * N]
    s = mx_kscale(D)[:, None]
    u = mx_kscale(N)
    ut = np.ones(T)
    ut[idx] = u
    kp = pack_weight(n((D, T)) / s, "e2m1")
    cp = pack_weight(n((D, T)) / s, "e2m1")
    return {
        "qT": (n((B, D, NQ)) * s * (1.00 / np.sqrt(D))).astype(np.float32),
        "k_words": np.ascontiguousarray(kp[0].reshape(1, 2, 128, T, 2).transpose(0, 2, 3, 1, 4)).reshape(1, 128, T, 4),
        "k_scales": kp[1],
        "c_words": np.ascontiguousarray(cp[0].reshape(1, 2, 128, T, 2).transpose(0, 2, 3, 1, 4)).reshape(1, 128, T, 4),
        "c_scales": cp[1],
        "vT": (n((DV, T)) / ut).astype(np.float32),
        "us": (sgn((B, N, 1)) * u[:, None]).astype(np.float32),
        "ob": (0.5 * n((B, 1, DV))).astype(np.float32),
        "offs": striped(idx),
    }


def reference(qT, k_words, k_scales, c_words, c_scales, vT, us, ob, offs):
    idx = unstriped(offs)
    pick = lambda x, which: x[:, which].reshape(x.shape[0], B, -1).transpose(1, 0, 2)
    k = unpack_weight(k_words.reshape(1, 128, T, 2, 2).transpose(0, 3, 1, 2, 4).reshape(2, 128, 2 * T), k_scales, "e2m1")
    kg = pick(k, idx)
    c = unpack_weight(c_words.reshape(1, 128, T, 2, 2).transpose(0, 3, 1, 2, 4).reshape(2, 128, 2 * T), c_scales, "e2m1")
    cg = pick(c, idx)
    qq = mxq(f64(qT), 1, "e4m3")
    a = kg.transpose(0, 2, 1) @ qq
    z = cg.transpose(0, 2, 1) @ qq
    y = np.maximum(a, 0.0) * z * f64(us)
    wq = mxq(y, 1, "e4m3")
    o = wq.transpose(0, 2, 1) @ mxq(pick(f64(vT), idx).transpose(0, 2, 1), 1, "e4m3")
    r_ = o + f64(ob)
    return r_

@@ -1,0 +1,207 @@
+from contextlib import ExitStack
+
+import concourse.mybir as mybir
+from concourse.masks import make_identity
+
+F32 = mybir.dt.float32
+BF16 = mybir.dt.bfloat16
+I32 = mybir.dt.int32
+U32 = mybir.dt.uint32
+U16 = mybir.dt.uint16
+U8 = mybir.dt.uint8
+FP8X4 = mybir.dt.float8_e4m3fn_x4
+FP4X4 = mybir.dt.float4_e2m1fn_x4
+ACT = mybir.ActivationFunctionType
+ALU = mybir.AluOpType
+
+P = 128
+PACK = 4
+SLOTS, NEURONS, FEATURES, QUERIES, OUTPUTS = 512, 2048, 1024, 512, 512
+PASSES = FEATURES // (P * PACK)
+HALF = QUERIES // 2
+
+FLOPS = 2 * 2 * SLOTS * FEATURES * QUERIES + 2 * SLOTS * QUERIES * OUTPUTS
+
+
+def interleave(copy, grouped, rows):
+    copy(
+        out=grouped.rearrange("p (c i) t -> p c t i", i=4),
+        in_=rows.rearrange("p t (c i) -> p c t i", i=4),
+    )
+
+
+def tile_attend_mlp_reglu_topk_kernel(tc, qT, k_words, k_scales, c_words, c_scales, vT, us, ob, offs, out):
+    nc = tc.nc
+    with ExitStack() as ctx:
+        keep = ctx.enter_context(tc.tile_pool(name="keep", bufs=1))
+        big = ctx.enter_context(tc.tile_pool(name="big", bufs=4))
+        ring = ctx.enter_context(tc.tile_pool(name="ring", bufs=2))
+        psum = ctx.enter_context(tc.psum_pool(name="psum", bufs=2))
+
+        offsets = keep.tile([P, SLOTS // 16], U16, name="offsets")
+        nc.sync.dma_start(offsets[:], offs)
+
+        scale_windows = []
+        for name, scales in (("k", k_scales), ("c", c_scales)):
+            window = keep.tile([P, NEURONS], U8, name=name + "_scale_window")
+            nc.vector.memset(window[32:64, :].bitcast(I32), 0)
+            nc.vector.memset(window[64:P, :].bitcast(I32), 0)
+            nc.scalar.dma_start(
+                out=window[0:32, :].bitcast(I32),
+                in_=scales.rearrange("o f t -> f o t").bitcast(I32),
+            )
+            scale_windows.append(window)
+        planes = keep.tile([P, PASSES, 2, SLOTS], U8, name="planes", align_bytes=64)
+        nc.vector.memset(planes[:].rearrange("p o w s -> p (o w s)").bitcast(I32), 0)
+
+        slot_scale = keep.tile([P, PACK], F32, name="slot_scale")
+        nc.scalar.dma_start(out=slot_scale[:], in_=us[0].rearrange("(p t) o -> p (t o)", t=PACK))
+        bias_columns = keep.tile([P, PACK], F32, name="bias_columns")
+        nc.scalar.dma_start(out=bias_columns[:], in_=ob[0].rearrange("o (p c) -> p (o c)", c=PACK))
+
+        q_rows = []
+        for o in range(PASSES):
+            rows = big.tile([P, PACK, QUERIES], F32, name="q_rows", tag="big")
+            nc.sync.dma_start(
+                out=rows[:], in_=qT[0, o * 512 : (o + 1) * 512, :].rearrange("(p t) q -> p t q", t=PACK)
+            )
+            q_rows.append(rows)
+        word_windows = []
+        for words in (k_words, c_words):
+            window = big.tile([P, NEURONS], U32, name="word_window", tag="big")
+            nc.sync.dma_start(
+                out=window[:].bitcast(I32), in_=words[0].rearrange("p t b -> p (t b)").bitcast(I32)
+            )
+            word_windows.append(window)
+
+        identity = keep.tile([P, P], F32, name="identity")
+        make_identity(nc, identity[:])
+
+        spread = psum.tile([P, PACK, P], F32, name="spread", tag="turn")
+        for c in range(PACK):
+            nc.tensor.transpose(spread[:, c, :], bias_columns[:, c : c + 1].to_broadcast([P, P]), identity[:])
+        bias = keep.tile([P, OUTPUTS], F32, name="bias")
+        nc.scalar.activation(
+            out=bias[:].rearrange("x (p c) -> x p c", c=PACK), in_=spread[:].rearrange("x c p -> x p c"), func=ACT.Copy
+        )
+
+        dealt_scales = keep.tile([P, 2, SLOTS], U8, name="dealt_scales")
+        for w in range(2):
+            picked = keep.tile([P, SLOTS], U8, name=f"picked_scales{w}")
+            nc.vector.tensor_copy(out=picked[:], in_=scale_windows[w][:].indirect(offsets[:]))
+            nc.vector.tensor_copy(
+                out=dealt_scales[:, w, :].rearrange("p (t s) -> p s t", t=PACK),
+                in_=picked[:].rearrange("p (s t) -> p s t", t=PACK),
+            )
+        for quadrant in range(4):
+            base = 32 * quadrant
+            nc.scalar.dma_start(
+                out=planes[base : base + 4].rearrange("p o w s -> p o (w s)").bitcast(I32),
+                in_=dealt_scales[8 * quadrant : 8 * quadrant + 8].rearrange("p w s -> p (w s)").bitcast(I32),
+            )
+
+        q_codes, q_scales = [], []
+        for o in range(PASSES):
+            grouped = keep.tile([P, QUERIES, PACK], BF16, name=f"q_grouped{o}", align_bytes=64)
+            interleave(nc.scalar.copy, grouped[:], q_rows[o][:])
+            codes = keep.tile([P, QUERIES], U32, name=f"q_codes{o}", align_bytes=64)
+            scales = keep.tile([P, QUERIES], U8, name=f"q_scales{o}", align_bytes=64)
+            nc.vector.quantize_mx(
+                out=codes[:].bitcast(FP8X4), scales=scales[:], in_=grouped[:].rearrange("p q t -> p (q t)")
+            )
+            q_codes.append(codes)
+            q_scales.append(scales)
+
+        def gather_words(w):
+            picked = keep.tile([P, SLOTS], U32, name=f"picked_words{w}")
+            nc.vector.tensor_copy(out=picked[:], in_=word_windows[w][:].indirect(offsets[:]))
+            halves = picked[:].bitcast(U16).rearrange("p (s t o) -> p o s t", t=PACK, o=PASSES)
+            dealt = []
+            for o in range(PASSES):
+                words = keep.tile([P, SLOTS], U16, name=f"dealt_words{w}{o}", align_bytes=64)
+                nc.vector.tensor_copy(out=words[:].rearrange("p (t s) -> p s t", t=PACK), in_=halves[:, o])
+                dealt.append(words)
+            return dealt
+
+        def scores(w, dealt, t):
+            bank = psum.tile([P, QUERIES], F32, name="score", tag="score", bufs=4)
+            cols = slice(t * P, (t + 1) * P)
+            for o in range(PASSES):
+                nc.tensor.matmul_mx(
+                    out=bank[:],
+                    lhsT=dealt[o][:, cols].bitcast(FP4X4),
+                    lhsT_scale=planes[:, o, w, cols],
+                    rhs=q_codes[o][:].bitcast(FP8X4),
+                    rhs_scale=q_scales[o][:],
+                    start=(o == 0),
+                    stop=(o == PASSES - 1),
+                )
+            return bank
+
+        gate = keep.tile([P, PACK, QUERIES], F32, name="gate")
+        k_dealt = gather_words(0)
+        for t in range(PACK):
+            nc.scalar.activation(out=gate[:, t, :], in_=scores(0, k_dealt, t)[:], func=ACT.Relu)
+
+        y_rows = keep.tile([P, PACK, QUERIES], BF16, name="y_rows")
+        c_dealt = gather_words(1)
+        for t in range(PACK):
+            nc.vector.scalar_tensor_tensor(
+                out=y_rows[:, t, :],
+                in0=scores(1, c_dealt, t)[:],
+                scalar=slot_scale[:, t : t + 1],
+                in1=gate[:, t, :],
+                op0=ALU.mult,
+                op1=ALU.mult,
+            )
+        y_codes, y_scales = [], []
+        for h, copy in enumerate((nc.vector.tensor_copy, nc.scalar.copy)):
+            grouped = keep.tile([P, HALF, PACK], BF16, name=f"y_grouped{h}", align_bytes=64)
+            interleave(copy, grouped[:], y_rows[:, :, h * HALF : (h + 1) * HALF])
+            codes = keep.tile([P, HALF], U32, name=f"y_codes{h}", align_bytes=64)
+            scales = keep.tile([P, HALF], U8, name=f"y_scales{h}", align_bytes=64)
+            nc.vector.quantize_mx(
+                out=codes[:].bitcast(FP8X4), scales=scales[:], in_=grouped[:].rearrange("p q t -> p (q t)")
+            )
+            y_codes.append(codes)
+            y_scales.append(scales)
+
+        for m in range(OUTPUTS // P):
+            cols = slice(m * P, (m + 1) * P)
+            window = big.tile([P, NEURONS], F32, name="v_window", tag="big")
+            nc.sync.dma_start(out=window[:], in_=vT[cols, :])
+            picked = ring.tile([P, SLOTS], BF16, name="v_picked")
+            nc.vector.tensor_copy(out=picked[:], in_=window[:].indirect(offsets[:]))
+            pairs = picked[:].bitcast(F32)
+            turned = psum.tile([P, 2, P], F32, name="turned", tag="turn")
+            for u in range(2):
+                nc.tensor.transpose(turned[:, u, :], pairs[:, u : 2 * P : 2], identity[:])
+            grouped = ring.tile([P, P, 2], F32, name="v_grouped", align_bytes=64)
+            nc.scalar.copy(out=grouped[:], in_=turned[:].rearrange("p u e -> p e u"))
+            codes = ring.tile([P, P], U32, name="v_codes", align_bytes=64, bufs=4)
+            scales = ring.tile([P, P], U8, name="v_scales", align_bytes=64, bufs=4)
+            nc.vector.quantize_mx(
+                out=codes[:].bitcast(FP8X4),
+                scales=scales[:],
+                in_=grouped[:].rearrange("p e u -> p (e u)").bitcast(BF16),
+            )
+            acc = psum.tile([P, QUERIES // P, P], F32, name="acc", tag="acc")
+            for j in range(QUERIES // P):
+                h, lo = divmod(j * P, HALF)
+                nc.tensor.matmul_mx(
+                    out=acc[:, j, :],
+                    lhsT=y_codes[h][:, lo : lo + P].bitcast(FP8X4),
+                    lhsT_scale=y_scales[h][:, lo : lo + P],
+                    rhs=codes[:].bitcast(FP8X4),
+                    rhs_scale=scales[:],
+                    start=True,
+                    stop=True,
+                )
+            result = ring.tile([P, QUERIES // P, P], F32, name="result", bufs=4)
+            nc.vector.tensor_tensor(
+                out=result[:],
+                in0=acc[:],
+                in1=bias[:, cols].unsqueeze(1).to_broadcast([P, QUERIES // P, P]),
+                op=ALU.add,
+            )
+            nc.sync.dma_start(out=out[0, :, cols].rearrange("(j p) e -> p j e", p=P), in_=result[:])

@@ -19,189 +19,229 @@ PACK = 4
 SLOTS, NEURONS, FEATURES, QUERIES, OUTPUTS = 512, 2048, 1024, 512, 512
 PASSES = FEATURES // (P * PACK)
 HALF = QUERIES // 2
+CHUNKS = OUTPUTS // P
 
 FLOPS = 2 * 2 * SLOTS * FEATURES * QUERIES + 2 * SLOTS * QUERIES * OUTPUTS
-
-
-def interleave(copy, grouped, rows):
-    copy(
-        out=grouped.rearrange("p (c i) t -> p c t i", i=4),
-        in_=rows.rearrange("p t (c i) -> p c t i", i=4),
-    )
 
 
 def tile_attend_mlp_reglu_topk_kernel(tc, qT, k_words, k_scales, c_words, c_scales, vT, us, ob, offs, out):
     nc = tc.nc
     with ExitStack() as ctx:
-        keep = ctx.enter_context(tc.tile_pool(name="keep", bufs=1))
-        big = ctx.enter_context(tc.tile_pool(name="big", bufs=4))
-        ring = ctx.enter_context(tc.tile_pool(name="ring", bufs=2))
-        psum = ctx.enter_context(tc.psum_pool(name="psum", bufs=2))
+        lists = ctx.enter_context(tc.tile_pool(name="lists", bufs=1))
+        sbuf = ctx.enter_context(tc.tile_pool(name="sbuf", bufs=1))
+        psum = ctx.enter_context(tc.psum_pool(name="psum", bufs=1))
 
-        offsets = keep.tile([P, SLOTS // 16], U16, name="offsets")
-        nc.sync.dma_start(offsets[:], offs)
+        def tile(name, shape, dtype, place=None):
+            return sbuf.tile(shape, dtype, name=name, tag=place or name, align_bytes=64)
 
-        scale_windows = []
-        for name, scales in (("k", k_scales), ("c", c_scales)):
-            window = keep.tile([P, NEURONS], U8, name=name + "_scale_window")
-            nc.vector.memset(window[32:64, :].bitcast(I32), 0)
-            nc.vector.memset(window[64:P, :].bitcast(I32), 0)
-            nc.scalar.dma_start(
-                out=window[0:32, :].bitcast(I32),
-                in_=scales.rearrange("o f t -> f o t").bitcast(I32),
+        def bank(name, shape, number):
+            return psum.tile(shape, F32, name=name, tag=f"bank{number}")
+
+        def scalar_cast(out, in_):
+            nc.scalar.activation(out=out, in_=in_, func=ACT.Copy)
+
+        def interleave(copy, grouped, rows):
+            copy(
+                out=grouped.rearrange("p (c i) t -> p c t i", i=4),
+                in_=rows.rearrange("p t (c i) -> p c t i", i=4),
             )
-            scale_windows.append(window)
-        planes = keep.tile([P, PASSES, 2, SLOTS], U8, name="planes", align_bytes=64)
-        nc.vector.memset(planes[:].rearrange("p o w s -> p (o w s)").bitcast(I32), 0)
 
-        slot_scale = keep.tile([P, PACK], F32, name="slot_scale")
+        def quantize(name, grouped, width):
+            codes = tile(name + "_codes", [P, width], U32)
+            scales = tile(name + "_scales", [P, width], U8)
+            nc.vector.quantize_mx(out=codes[:].bitcast(FP8X4), scales=scales[:], in_=grouped)
+            return codes, scales
+
+        def load_scales(name, scales, memset):
+            window = tile(name, [P, NEURONS], U8)
+            memset(window[32:64, :].bitcast(I32), 0)
+            memset(window[64:P, :].bitcast(I32), 0)
+            nc.sync.dma_start(out=window[0:32, :].bitcast(I32), in_=scales.rearrange("o f t -> f o t").bitcast(I32))
+            return window
+
+        def load_q(o, place):
+            rows = tile(f"q_rows{o}", [P, PACK, QUERIES], F32, place)
+            nc.sync.dma_start(out=rows[:], in_=qT[0, o * 512 : (o + 1) * 512, :].rearrange("(p t) q -> p t q", t=PACK))
+            return rows
+
+        def load_words(name, words, place):
+            window = tile(name, [P, NEURONS], U32, place)
+            nc.sync.dma_start(out=window[:].bitcast(I32), in_=words[0].rearrange("p t b -> p (t b)").bitcast(I32))
+            return window
+
+        def load_v(m, place):
+            window = tile(f"v_window{m}", [P, NEURONS], F32, place)
+            nc.sync.dma_start(out=window[:], in_=vT[m * P : (m + 1) * P, :])
+            return window
+
+        k_scale_window = load_scales("k_scale_window", k_scales, nc.vector.memset)
+        offsets = lists.tile([P, SLOTS // 16], U16, name="offsets")
+        nc.sync.dma_start(offsets[:], offs)
+        c_scale_window = load_scales("c_scale_window", c_scales, nc.gpsimd.memset)
+        q_rows0 = load_q(0, "A")
+        k_window = load_words("k_window", k_words, "E")
+        q_rows1 = load_q(1, "C")
+
+        slot_scale = tile("slot_scale", [P, PACK], F32)
         nc.scalar.dma_start(out=slot_scale[:], in_=us[0].rearrange("(p t) o -> p (t o)", t=PACK))
-        bias_columns = keep.tile([P, PACK], F32, name="bias_columns")
+        bias_columns = tile("bias_columns", [P, PACK], F32)
         nc.scalar.dma_start(out=bias_columns[:], in_=ob[0].rearrange("o (p c) -> p (o c)", c=PACK))
 
-        q_rows = []
-        for o in range(PASSES):
-            rows = big.tile([P, PACK, QUERIES], F32, name="q_rows", tag="big")
-            nc.sync.dma_start(
-                out=rows[:], in_=qT[0, o * 512 : (o + 1) * 512, :].rearrange("(p t) q -> p t q", t=PACK)
-            )
-            q_rows.append(rows)
-        word_windows = []
-        for words in (k_words, c_words):
-            window = big.tile([P, NEURONS], U32, name="word_window", tag="big")
-            nc.sync.dma_start(
-                out=window[:].bitcast(I32), in_=words[0].rearrange("p t b -> p (t b)").bitcast(I32)
-            )
-            word_windows.append(window)
-
-        identity = keep.tile([P, P], F32, name="identity")
+        planes = tile("planes", [P, PASSES, 2, SLOTS], U8)
+        nc.vector.memset(planes[:].rearrange("p o w s -> p (o w s)").bitcast(I32), 0)
+        identity = tile("identity", [P, P], F32)
         make_identity(nc, identity[:])
 
-        spread = psum.tile([P, PACK, P], F32, name="spread", tag="turn")
-        for c in range(PACK):
-            nc.tensor.transpose(spread[:, c, :], bias_columns[:, c : c + 1].to_broadcast([P, P]), identity[:])
-        bias = keep.tile([P, OUTPUTS], F32, name="bias")
-        nc.scalar.activation(
-            out=bias[:].rearrange("x (p c) -> x p c", c=PACK), in_=spread[:].rearrange("x c p -> x p c"), func=ACT.Copy
-        )
-
-        dealt_scales = keep.tile([P, 2, SLOTS], U8, name="dealt_scales")
-        for w in range(2):
-            picked = keep.tile([P, SLOTS], U8, name=f"picked_scales{w}")
-            nc.vector.tensor_copy(out=picked[:], in_=scale_windows[w][:].indirect(offsets[:]))
+        dealt_scales = tile("dealt_scales", [P, 2, SLOTS], U8)
+        for w, window in enumerate((k_scale_window, c_scale_window)):
+            picked = tile(f"picked_scales{w}", [P, SLOTS], U8, ("F", "D")[w])
+            nc.vector.tensor_copy(out=picked[:], in_=window[:].indirect(offsets[:]))
             nc.vector.tensor_copy(
-                out=dealt_scales[:, w, :].rearrange("p (t s) -> p s t", t=PACK),
-                in_=picked[:].rearrange("p (s t) -> p s t", t=PACK),
+                out=dealt_scales[:, w, :].rearrange("p (t s) -> p t s", t=PACK),
+                in_=picked[:].rearrange("p (s t) -> p t s", t=PACK),
             )
+
+        q_grouped0 = tile("q_grouped0", [P, QUERIES, PACK], BF16, "B")
+        interleave(scalar_cast, q_grouped0[:], q_rows0[:])
         for quadrant in range(4):
-            base = 32 * quadrant
-            nc.scalar.dma_start(
-                out=planes[base : base + 4].rearrange("p o w s -> p o (w s)").bitcast(I32),
+            nc.sync.dma_start(
+                out=planes[32 * quadrant : 32 * quadrant + 4].rearrange("p o w s -> p o (w s)").bitcast(I32),
                 in_=dealt_scales[8 * quadrant : 8 * quadrant + 8].rearrange("p w s -> p (w s)").bitcast(I32),
             )
+        c_window = load_words("c_window", c_words, "D")
 
-        q_codes, q_scales = [], []
-        for o in range(PASSES):
-            grouped = keep.tile([P, QUERIES, PACK], BF16, name=f"q_grouped{o}", align_bytes=64)
-            interleave(nc.scalar.copy, grouped[:], q_rows[o][:])
-            codes = keep.tile([P, QUERIES], U32, name=f"q_codes{o}", align_bytes=64)
-            scales = keep.tile([P, QUERIES], U8, name=f"q_scales{o}", align_bytes=64)
-            nc.vector.quantize_mx(
-                out=codes[:].bitcast(FP8X4), scales=scales[:], in_=grouped[:].rearrange("p q t -> p (q t)")
-            )
-            q_codes.append(codes)
-            q_scales.append(scales)
-
-        def gather_words(w):
-            picked = keep.tile([P, SLOTS], U32, name=f"picked_words{w}")
-            nc.vector.tensor_copy(out=picked[:], in_=word_windows[w][:].indirect(offsets[:]))
+        def gather_words(w, window):
+            picked = tile(f"picked_words{w}", [P, SLOTS], U32, "X")
+            nc.vector.tensor_copy(out=picked[:], in_=window[:].indirect(offsets[:]))
             halves = picked[:].bitcast(U16).rearrange("p (s t o) -> p o s t", t=PACK, o=PASSES)
             dealt = []
             for o in range(PASSES):
-                words = keep.tile([P, SLOTS], U16, name=f"dealt_words{w}{o}", align_bytes=64)
+                words = tile(f"dealt_words{w}{o}", [P, SLOTS], U16)
                 nc.vector.tensor_copy(out=words[:].rearrange("p (t s) -> p s t", t=PACK), in_=halves[:, o])
                 dealt.append(words)
             return dealt
 
-        def scores(w, dealt, t):
-            bank = psum.tile([P, QUERIES], F32, name="score", tag="score", bufs=4)
+        def score_pass(acc, w, dealt, t, o):
             cols = slice(t * P, (t + 1) * P)
-            for o in range(PASSES):
-                nc.tensor.matmul_mx(
-                    out=bank[:],
-                    lhsT=dealt[o][:, cols].bitcast(FP4X4),
-                    lhsT_scale=planes[:, o, w, cols],
-                    rhs=q_codes[o][:].bitcast(FP8X4),
-                    rhs_scale=q_scales[o][:],
-                    start=(o == 0),
-                    stop=(o == PASSES - 1),
-                )
-            return bank
-
-        gate = keep.tile([P, PACK, QUERIES], F32, name="gate")
-        k_dealt = gather_words(0)
-        for t in range(PACK):
-            nc.scalar.activation(out=gate[:, t, :], in_=scores(0, k_dealt, t)[:], func=ACT.Relu)
-
-        y_rows = keep.tile([P, PACK, QUERIES], BF16, name="y_rows")
-        c_dealt = gather_words(1)
-        for t in range(PACK):
-            nc.vector.scalar_tensor_tensor(
-                out=y_rows[:, t, :],
-                in0=scores(1, c_dealt, t)[:],
-                scalar=slot_scale[:, t : t + 1],
-                in1=gate[:, t, :],
-                op0=ALU.mult,
-                op1=ALU.mult,
+            nc.tensor.matmul_mx(
+                out=acc[:],
+                lhsT=dealt[o][:, cols].bitcast(FP4X4),
+                lhsT_scale=planes[:, o, w, cols],
+                rhs=q[o][0][:].bitcast(FP8X4),
+                rhs_scale=q[o][1][:],
+                start=(o == 0),
+                stop=(o == PASSES - 1),
             )
-        y_codes, y_scales = [], []
-        for h, copy in enumerate((nc.vector.tensor_copy, nc.scalar.copy)):
-            grouped = keep.tile([P, HALF, PACK], BF16, name=f"y_grouped{h}", align_bytes=64)
-            interleave(copy, grouped[:], y_rows[:, :, h * HALF : (h + 1) * HALF])
-            codes = keep.tile([P, HALF], U32, name=f"y_codes{h}", align_bytes=64)
-            scales = keep.tile([P, HALF], U8, name=f"y_scales{h}", align_bytes=64)
+
+        v_windows = [load_v(0, "A")]
+        k_dealt = gather_words(0, k_window)
+        q = [quantize("q0", q_grouped0[:].rearrange("p q t -> p (q t)"), QUERIES)]
+        v_windows.append(load_v(1, "B"))
+        a = [bank(f"a{t}", [P, QUERIES], t) for t in range(PACK)]
+        for t in range(PACK):
+            score_pass(a[t], 0, k_dealt, t, 0)
+
+        spread = bank("spread", [P, PACK, P], 7)
+        for c in range(PACK):
+            nc.tensor.transpose(spread[:, c, :], bias_columns[:, c : c + 1].to_broadcast([P, P]), identity[:])
+        bias = tile("bias", [P, OUTPUTS], F32, "E")
+        scalar_cast(bias[:].rearrange("x (p c) -> x p c", c=PACK), spread[:].rearrange("x c p -> x p c"))
+
+        q1_low = tile("q1_low", [P, HALF, PACK], BF16, "X")
+        q1_high = tile("q1_high", [P, HALF, PACK], BF16)
+        interleave(nc.vector.tensor_copy, q1_low[:], q_rows1[:, :, 0:HALF])
+        interleave(scalar_cast, q1_high[:], q_rows1[:, :, HALF:QUERIES])
+        v_windows.append(load_v(2, "C"))
+        q1_codes = tile("q1_codes", [P, QUERIES], U32)
+        q1_scales = tile("q1_scales", [P, QUERIES], U8)
+        for lo, grouped in ((HALF, q1_high), (0, q1_low)):
             nc.vector.quantize_mx(
-                out=codes[:].bitcast(FP8X4), scales=scales[:], in_=grouped[:].rearrange("p q t -> p (q t)")
+                out=q1_codes[:, lo : lo + HALF].bitcast(FP8X4),
+                scales=q1_scales[:, lo : lo + HALF],
+                in_=grouped[:].rearrange("p q t -> p (q t)"),
             )
-            y_codes.append(codes)
-            y_scales.append(scales)
+        q.append((q1_codes, q1_scales))
+        gates = []
+        for t in range(PACK):
+            score_pass(a[t], 0, k_dealt, t, 1)
+            gate = tile(f"gate{t}", [P, QUERIES], F32)
+            nc.scalar.activation(out=gate[:], in_=a[t][:], func=ACT.Relu)
+            gates.append(gate)
 
-        for m in range(OUTPUTS // P):
-            cols = slice(m * P, (m + 1) * P)
-            window = big.tile([P, NEURONS], F32, name="v_window", tag="big")
-            nc.sync.dma_start(out=window[:], in_=vT[cols, :])
-            picked = ring.tile([P, SLOTS], BF16, name="v_picked")
-            nc.vector.tensor_copy(out=picked[:], in_=window[:].indirect(offsets[:]))
+        c_dealt = gather_words(1, c_window)
+        v_windows.append(load_v(3, "D"))
+
+        def gather_v(m, place):
+            picked = tile(f"v_picked{m}", [P, SLOTS], BF16, place)
+            nc.vector.tensor_copy(out=picked[:], in_=v_windows[m][:].indirect(offsets[:]))
+            return picked
+
+        def turn_v(m, picked, grouped):
             pairs = picked[:].bitcast(F32)
-            turned = psum.tile([P, 2, P], F32, name="turned", tag="turn")
+            turned = bank(f"turned{m}", [P, 2, P], PACK + m)
             for u in range(2):
                 nc.tensor.transpose(turned[:, u, :], pairs[:, u : 2 * P : 2], identity[:])
-            grouped = ring.tile([P, P, 2], F32, name="v_grouped", align_bytes=64)
-            nc.scalar.copy(out=grouped[:], in_=turned[:].rearrange("p u e -> p e u"))
-            codes = ring.tile([P, P], U32, name="v_codes", align_bytes=64, bufs=4)
-            scales = ring.tile([P, P], U8, name="v_scales", align_bytes=64, bufs=4)
+            nc.scalar.copy(out=grouped, in_=turned[:].rearrange("p u e -> p e u"))
+
+        picked0 = gather_v(0, "q1_high")
+        y_rows = tile("y_rows", [P, PACK, QUERIES], BF16, "A")
+        for t in range(PACK):
+            z = bank(f"z{t}", [P, QUERIES], PACK + t)
+            for o in range(PASSES):
+                score_pass(z, 1, c_dealt, t, o)
+            nc.vector.scalar_tensor_tensor(
+                out=y_rows[:, t, :], in0=z[:], scalar=slot_scale[:, t : t + 1], in1=gates[t][:], op0=ALU.mult, op1=ALU.mult
+            )
+        picked1 = gather_v(1, "gate2")
+        picked2 = gather_v(2, "gate3")
+        y = []
+        for h in range(2):
+            grouped = tile(f"y_grouped{h}", [P, HALF, PACK], BF16)
+            interleave(nc.scalar.copy, grouped[:], y_rows[:, :, h * HALF : (h + 1) * HALF])
+            y.append(quantize(f"y{h}", grouped[:].rearrange("p q t -> p (q t)"), HALF))
+        v0_grouped = tile("v0_grouped", [P, P, 2], F32)
+        turn_v(0, picked0, v0_grouped[:])
+        picked3 = gather_v(3, "y_grouped0")
+        v12_grouped = tile("v12_grouped", [P, 2 * P, 2], F32, "A")
+        turn_v(1, picked1, v12_grouped[:, 0:P, :])
+        turn_v(2, picked2, v12_grouped[:, P : 2 * P, :])
+        v3_grouped = tile("v3_grouped", [P, P, 2], F32)
+        turn_v(3, picked3, v3_grouped[:])
+        v_codes = tile("v_codes", [P, OUTPUTS], U32, "D")
+        v_scales = tile("v_scales", [P, OUTPUTS], U8)
+        for first, width, grouped in ((0, P, v0_grouped), (P, 2 * P, v12_grouped), (3 * P, P, v3_grouped)):
             nc.vector.quantize_mx(
-                out=codes[:].bitcast(FP8X4),
-                scales=scales[:],
+                out=v_codes[:, first : first + width].bitcast(FP8X4),
+                scales=v_scales[:, first : first + width],
                 in_=grouped[:].rearrange("p e u -> p (e u)").bitcast(BF16),
             )
-            acc = psum.tile([P, QUERIES // P, P], F32, name="acc", tag="acc")
-            for j in range(QUERIES // P):
+
+        def finish(number, first, width, q_tiles, queue):
+            cols = slice(first, first + width)
+            acc = bank(f"acc{number}", [P, len(q_tiles), width], number)
+            for n, j in enumerate(q_tiles):
                 h, lo = divmod(j * P, HALF)
                 nc.tensor.matmul_mx(
-                    out=acc[:, j, :],
-                    lhsT=y_codes[h][:, lo : lo + P].bitcast(FP8X4),
-                    lhsT_scale=y_scales[h][:, lo : lo + P],
-                    rhs=codes[:].bitcast(FP8X4),
-                    rhs_scale=scales[:],
+                    out=acc[:, n, :],
+                    lhsT=y[h][0][:, lo : lo + P].bitcast(FP8X4),
+                    lhsT_scale=y[h][1][:, lo : lo + P],
+                    rhs=v_codes[:, cols].bitcast(FP8X4),
+                    rhs_scale=v_scales[:, cols],
                     start=True,
                     stop=True,
                 )
-            result = ring.tile([P, QUERIES // P, P], F32, name="result", bufs=4)
+            result = tile(f"result{number}", [P, len(q_tiles), width], F32)[:]
             nc.vector.tensor_tensor(
-                out=result[:],
+                out=result,
                 in0=acc[:],
-                in1=bias[:, cols].unsqueeze(1).to_broadcast([P, QUERIES // P, P]),
+                in1=bias[:, cols].unsqueeze(1).to_broadcast([P, len(q_tiles), width]),
                 op=ALU.add,
             )
-            nc.sync.dma_start(out=out[0, :, cols].rearrange("(j p) e -> p j e", p=P), in_=result[:])
+            rows = out[0, q_tiles[0] * P : (q_tiles[-1] + 1) * P, cols]
+            queue.dma_start(out=rows.rearrange("(j p) e -> p j e", p=P), in_=result)
+
+        finish(0, 0, P, [0, 1, 2, 3], nc.sync)
+        finish(1, P, 2 * P, [0, 1], nc.sync)
+        finish(2, P, 2 * P, [2, 3], nc.sync)
+        finish(3, 3 * P, P, [0, 1], nc.scalar)
+        finish(4, 3 * P, P, [2, 3], nc.sync)

@@ -17,11 +17,14 @@ ALU = mybir.AluOpType
 P = 128
 PACK = 4
 SLOTS, NEURONS, FEATURES, QUERIES, OUTPUTS = 512, 2048, 1024, 512, 512
-PASSES = FEATURES // (P * PACK)
+K_PASS = P * PACK
+PASSES = FEATURES // K_PASS
+TABLES = 2
+SCALE_ROWS = FEATURES // 32
 HALF = QUERIES // 2
-CHUNKS = OUTPUTS // P
+LINE = 4
 
-FLOPS = 2 * 2 * SLOTS * FEATURES * QUERIES + 2 * SLOTS * QUERIES * OUTPUTS
+FLOPS = 2 * TABLES * SLOTS * FEATURES * QUERIES + 2 * SLOTS * QUERIES * OUTPUTS
 
 
 def tile_attend_mlp_reglu_topk_kernel(tc, qT, k_words, k_scales, c_words, c_scales, vT, us, ob, offs, out):
@@ -31,46 +34,49 @@ def tile_attend_mlp_reglu_topk_kernel(tc, qT, k_words, k_scales, c_words, c_scal
         sbuf = ctx.enter_context(tc.tile_pool(name="sbuf", bufs=1))
         psum = ctx.enter_context(tc.psum_pool(name="psum", bufs=1))
 
-        def tile(name, shape, dtype, place=None):
-            return sbuf.tile(shape, dtype, name=name, tag=place or name, align_bytes=64)
+        def tile(name, shape, dtype, reuse=None):
+            return sbuf.tile(shape, dtype, name=name, tag=reuse or name, align_bytes=64)
 
         def bank(name, shape, number):
             return psum.tile(shape, F32, name=name, tag=f"bank{number}")
 
-        def scalar_cast(out, in_):
+        def scalar_move(out, in_):
             nc.scalar.activation(out=out, in_=in_, func=ACT.Copy)
 
-        def interleave(copy, grouped, rows):
-            copy(
-                out=grouped.rearrange("p (c i) t -> p c t i", i=4),
-                in_=rows.rearrange("p t (c i) -> p c t i", i=4),
+        def interleave(move, grouped, rows):
+            move(
+                out=grouped.rearrange("p (c i) t -> p c t i", i=LINE),
+                in_=rows.rearrange("p t (c i) -> p c t i", i=LINE),
             )
 
-        def quantize(name, grouped, width):
-            codes = tile(name + "_codes", [P, width], U32)
-            scales = tile(name + "_scales", [P, width], U8)
-            nc.vector.quantize_mx(out=codes[:].bitcast(FP8X4), scales=scales[:], in_=grouped)
-            return codes, scales
+        def quantize(codes, scales, grouped):
+            nc.vector.quantize_mx(out=codes.bitcast(FP8X4), scales=scales, in_=grouped)
+
+        def flat(grouped):
+            return grouped[:].rearrange("p c t -> p (c t)")
 
         def load_scales(name, scales, memset):
             window = tile(name, [P, NEURONS], U8)
-            memset(window[32:64, :].bitcast(I32), 0)
+            memset(window[SCALE_ROWS:64, :].bitcast(I32), 0)
             memset(window[64:P, :].bitcast(I32), 0)
-            nc.sync.dma_start(out=window[0:32, :].bitcast(I32), in_=scales.rearrange("o f t -> f o t").bitcast(I32))
+            nc.sync.dma_start(
+                out=window[0:SCALE_ROWS, :].bitcast(I32), in_=scales.rearrange("o f n -> f o n").bitcast(I32)
+            )
             return window
 
-        def load_q(o, place):
-            rows = tile(f"q_rows{o}", [P, PACK, QUERIES], F32, place)
-            nc.sync.dma_start(out=rows[:], in_=qT[0, o * 512 : (o + 1) * 512, :].rearrange("(p t) q -> p t q", t=PACK))
+        def load_queries(o):
+            rows = tile(f"q_rows{o}", [P, PACK, QUERIES], F32)
+            features = qT[0, o * K_PASS : (o + 1) * K_PASS, :]
+            nc.sync.dma_start(out=rows[:], in_=features.rearrange("(p t) q -> p t q", t=PACK))
             return rows
 
-        def load_words(name, words, place):
-            window = tile(name, [P, NEURONS], U32, place)
-            nc.sync.dma_start(out=window[:].bitcast(I32), in_=words[0].rearrange("p t b -> p (t b)").bitcast(I32))
+        def load_words(name, words, reuse=None):
+            window = tile(name, [P, NEURONS], U32, reuse)
+            nc.sync.dma_start(out=window[:].bitcast(I32), in_=words[0].rearrange("p n b -> p (n b)").bitcast(I32))
             return window
 
-        def load_v(m, place):
-            window = tile(f"v_window{m}", [P, NEURONS], F32, place)
+        def load_values(m, reuse):
+            window = tile(f"v_window{m}", [P, NEURONS], F32, reuse)
             nc.sync.dma_start(out=window[:], in_=vT[m * P : (m + 1) * P, :])
             return window
 
@@ -78,42 +84,43 @@ def tile_attend_mlp_reglu_topk_kernel(tc, qT, k_words, k_scales, c_words, c_scal
         offsets = lists.tile([P, SLOTS // 16], U16, name="offsets")
         nc.sync.dma_start(offsets[:], offs)
         c_scale_window = load_scales("c_scale_window", c_scales, nc.gpsimd.memset)
-        q_rows0 = load_q(0, "A")
-        k_window = load_words("k_window", k_words, "E")
-        q_rows1 = load_q(1, "C")
+        q_rows0 = load_queries(0)
+        k_window = load_words("k_window", k_words)
+        q_rows1 = load_queries(1)
 
         slot_scale = tile("slot_scale", [P, PACK], F32)
         nc.scalar.dma_start(out=slot_scale[:], in_=us[0].rearrange("(p t) o -> p (t o)", t=PACK))
         bias_columns = tile("bias_columns", [P, PACK], F32)
         nc.scalar.dma_start(out=bias_columns[:], in_=ob[0].rearrange("o (p c) -> p (o c)", c=PACK))
 
-        planes = tile("planes", [P, PASSES, 2, SLOTS], U8)
+        planes = tile("planes", [P, PASSES, TABLES, SLOTS], U8)
         nc.vector.memset(planes[:].rearrange("p o w s -> p (o w s)").bitcast(I32), 0)
         identity = tile("identity", [P, P], F32)
         make_identity(nc, identity[:])
 
-        dealt_scales = tile("dealt_scales", [P, 2, SLOTS], U8)
+        dealt_scales = tile("dealt_scales", [P, TABLES, SLOTS], U8)
         for w, window in enumerate((k_scale_window, c_scale_window)):
-            picked = tile(f"picked_scales{w}", [P, SLOTS], U8, ("F", "D")[w])
-            nc.vector.tensor_copy(out=picked[:], in_=window[:].indirect(offsets[:]))
+            picked_scales = tile(f"picked_scales{w}", [P, SLOTS], U8)
+            nc.vector.tensor_copy(out=picked_scales[:], in_=window[:].indirect(offsets[:]))
             nc.vector.tensor_copy(
                 out=dealt_scales[:, w, :].rearrange("p (t s) -> p t s", t=PACK),
-                in_=picked[:].rearrange("p (s t) -> p t s", t=PACK),
+                in_=picked_scales[:].rearrange("p (s t) -> p t s", t=PACK),
             )
 
-        q_grouped0 = tile("q_grouped0", [P, QUERIES, PACK], BF16, "B")
-        interleave(scalar_cast, q_grouped0[:], q_rows0[:])
-        for quadrant in range(4):
+        q_grouped0 = tile("q_grouped0", [P, QUERIES, PACK], BF16)
+        interleave(scalar_move, q_grouped0[:], q_rows0[:])
+
+        for n in range(4):
             nc.sync.dma_start(
-                out=planes[32 * quadrant : 32 * quadrant + 4].rearrange("p o w s -> p o (w s)").bitcast(I32),
-                in_=dealt_scales[8 * quadrant : 8 * quadrant + 8].rearrange("p w s -> p (w s)").bitcast(I32),
+                out=planes[32 * n : 32 * n + 4].rearrange("p o w s -> p o (w s)").bitcast(I32),
+                in_=dealt_scales[8 * n : 8 * n + 8].rearrange("p w s -> p (w s)").bitcast(I32),
             )
-        c_window = load_words("c_window", c_words, "D")
+        c_window = load_words("c_window", c_words, reuse="picked_scales1")
 
         def gather_words(w, window):
-            picked = tile(f"picked_words{w}", [P, SLOTS], U32, "X")
-            nc.vector.tensor_copy(out=picked[:], in_=window[:].indirect(offsets[:]))
-            halves = picked[:].bitcast(U16).rearrange("p (s t o) -> p o s t", t=PACK, o=PASSES)
+            picked_words = tile(f"picked_words{w}", [P, SLOTS], U32, reuse="picked_words0")
+            nc.vector.tensor_copy(out=picked_words[:], in_=window[:].indirect(offsets[:]))
+            halves = picked_words[:].bitcast(U16).rearrange("p (s t o) -> p o s t", t=PACK, o=PASSES)
             dealt = []
             for o in range(PASSES):
                 words = tile(f"dealt_words{w}{o}", [P, SLOTS], U16)
@@ -121,46 +128,46 @@ def tile_attend_mlp_reglu_topk_kernel(tc, qT, k_words, k_scales, c_words, c_scal
                 dealt.append(words)
             return dealt
 
+        q_codes, q_scales = [], []
+
         def score_pass(acc, w, dealt, t, o):
             cols = slice(t * P, (t + 1) * P)
             nc.tensor.matmul_mx(
                 out=acc[:],
                 lhsT=dealt[o][:, cols].bitcast(FP4X4),
                 lhsT_scale=planes[:, o, w, cols],
-                rhs=q[o][0][:].bitcast(FP8X4),
-                rhs_scale=q[o][1][:],
+                rhs=q_codes[o][:].bitcast(FP8X4),
+                rhs_scale=q_scales[o][:],
                 start=(o == 0),
                 stop=(o == PASSES - 1),
             )
 
-        v_windows = [load_v(0, "A")]
+        v_windows = [load_values(0, reuse="q_rows0")]
         k_dealt = gather_words(0, k_window)
-        q = [quantize("q0", q_grouped0[:].rearrange("p q t -> p (q t)"), QUERIES)]
-        v_windows.append(load_v(1, "B"))
+        q_codes.append(tile("q_codes0", [P, QUERIES], U32))
+        q_scales.append(tile("q_scales0", [P, QUERIES], U8))
+        quantize(q_codes[0][:], q_scales[0][:], flat(q_grouped0))
+        v_windows.append(load_values(1, reuse="q_grouped0"))
+
         a = [bank(f"a{t}", [P, QUERIES], t) for t in range(PACK)]
         for t in range(PACK):
             score_pass(a[t], 0, k_dealt, t, 0)
 
-        spread = bank("spread", [P, PACK, P], 7)
+        spread = bank("spread", [P, PACK, P], 2 * PACK - 1)
         for c in range(PACK):
             nc.tensor.transpose(spread[:, c, :], bias_columns[:, c : c + 1].to_broadcast([P, P]), identity[:])
-        bias = tile("bias", [P, OUTPUTS], F32, "E")
-        scalar_cast(bias[:].rearrange("x (p c) -> x p c", c=PACK), spread[:].rearrange("x c p -> x p c"))
+        bias = tile("bias", [P, OUTPUTS], F32, reuse="k_window")
+        scalar_move(bias[:].rearrange("x (p c) -> x p c", c=PACK), spread[:].rearrange("x c p -> x p c"))
 
-        q1_low = tile("q1_low", [P, HALF, PACK], BF16, "X")
+        q1_low = tile("q1_low", [P, HALF, PACK], BF16, reuse="picked_words0")
         q1_high = tile("q1_high", [P, HALF, PACK], BF16)
         interleave(nc.vector.tensor_copy, q1_low[:], q_rows1[:, :, 0:HALF])
-        interleave(scalar_cast, q1_high[:], q_rows1[:, :, HALF:QUERIES])
-        v_windows.append(load_v(2, "C"))
-        q1_codes = tile("q1_codes", [P, QUERIES], U32)
-        q1_scales = tile("q1_scales", [P, QUERIES], U8)
-        for lo, grouped in ((HALF, q1_high), (0, q1_low)):
-            nc.vector.quantize_mx(
-                out=q1_codes[:, lo : lo + HALF].bitcast(FP8X4),
-                scales=q1_scales[:, lo : lo + HALF],
-                in_=grouped[:].rearrange("p q t -> p (q t)"),
-            )
-        q.append((q1_codes, q1_scales))
+        interleave(scalar_move, q1_high[:], q_rows1[:, :, HALF:QUERIES])
+        v_windows.append(load_values(2, reuse="q_rows1"))
+        q_codes.append(tile("q_codes1", [P, QUERIES], U32))
+        q_scales.append(tile("q_scales1", [P, QUERIES], U8))
+        quantize(q_codes[1][:, HALF:QUERIES], q_scales[1][:, HALF:QUERIES], flat(q1_high))
+        quantize(q_codes[1][:, 0:HALF], q_scales[1][:, 0:HALF], flat(q1_low))
         gates = []
         for t in range(PACK):
             score_pass(a[t], 0, k_dealt, t, 1)
@@ -169,52 +176,61 @@ def tile_attend_mlp_reglu_topk_kernel(tc, qT, k_words, k_scales, c_words, c_scal
             gates.append(gate)
 
         c_dealt = gather_words(1, c_window)
-        v_windows.append(load_v(3, "D"))
+        v_windows.append(load_values(3, reuse="picked_scales1"))
 
-        def gather_v(m, place):
-            picked = tile(f"v_picked{m}", [P, SLOTS], BF16, place)
-            nc.vector.tensor_copy(out=picked[:], in_=v_windows[m][:].indirect(offsets[:]))
-            return picked
+        def gather_values(m, reuse):
+            picked_values = tile(f"picked_values{m}", [P, SLOTS], BF16, reuse)
+            nc.vector.tensor_copy(out=picked_values[:], in_=v_windows[m][:].indirect(offsets[:]))
+            return picked_values
 
-        def turn_v(m, picked, grouped):
-            pairs = picked[:].bitcast(F32)
+        def turn_values(m, picked_values, grouped):
+            pairs = picked_values[:].bitcast(F32)
             turned = bank(f"turned{m}", [P, 2, P], PACK + m)
             for u in range(2):
                 nc.tensor.transpose(turned[:, u, :], pairs[:, u : 2 * P : 2], identity[:])
             nc.scalar.copy(out=grouped, in_=turned[:].rearrange("p u e -> p e u"))
 
-        picked0 = gather_v(0, "q1_high")
-        y_rows = tile("y_rows", [P, PACK, QUERIES], BF16, "A")
+        picked0 = gather_values(0, reuse="q1_high")
+        y_rows = tile("y_rows", [P, PACK, QUERIES], BF16, reuse="q_rows0")
         for t in range(PACK):
             z = bank(f"z{t}", [P, QUERIES], PACK + t)
             for o in range(PASSES):
                 score_pass(z, 1, c_dealt, t, o)
             nc.vector.scalar_tensor_tensor(
-                out=y_rows[:, t, :], in0=z[:], scalar=slot_scale[:, t : t + 1], in1=gates[t][:], op0=ALU.mult, op1=ALU.mult
+                out=y_rows[:, t, :],
+                in0=z[:],
+                scalar=slot_scale[:, t : t + 1],
+                in1=gates[t][:],
+                op0=ALU.mult,
+                op1=ALU.mult,
             )
-        picked1 = gather_v(1, "gate2")
-        picked2 = gather_v(2, "gate3")
-        y = []
+        picked1 = gather_values(1, reuse="gate2")
+        picked2 = gather_values(2, reuse="gate3")
+        y_grouped = []
         for h in range(2):
-            grouped = tile(f"y_grouped{h}", [P, HALF, PACK], BF16)
-            interleave(nc.scalar.copy, grouped[:], y_rows[:, :, h * HALF : (h + 1) * HALF])
-            y.append(quantize(f"y{h}", grouped[:].rearrange("p q t -> p (q t)"), HALF))
+            y_grouped.append(tile(f"y_grouped{h}", [P, HALF, PACK], BF16))
+            interleave(nc.scalar.copy, y_grouped[h][:], y_rows[:, :, h * HALF : (h + 1) * HALF])
+        y0_codes = tile("y0_codes", [P, HALF], U32)
+        y0_scales = tile("y0_scales", [P, HALF], U8)
+        quantize(y0_codes[:], y0_scales[:], flat(y_grouped[0]))
         v0_grouped = tile("v0_grouped", [P, P, 2], F32)
-        turn_v(0, picked0, v0_grouped[:])
-        picked3 = gather_v(3, "y_grouped0")
-        v12_grouped = tile("v12_grouped", [P, 2 * P, 2], F32, "A")
-        turn_v(1, picked1, v12_grouped[:, 0:P, :])
-        turn_v(2, picked2, v12_grouped[:, P : 2 * P, :])
+        turn_values(0, picked0, v0_grouped[:])
+        picked3 = gather_values(3, reuse="y_grouped0")
+        v12_grouped = tile("v12_grouped", [P, 2 * P, 2], F32, reuse="q_rows0")
+        turn_values(1, picked1, v12_grouped[:, 0:P, :])
+        turn_values(2, picked2, v12_grouped[:, P : 2 * P, :])
         v3_grouped = tile("v3_grouped", [P, P, 2], F32)
-        turn_v(3, picked3, v3_grouped[:])
-        v_codes = tile("v_codes", [P, OUTPUTS], U32, "D")
+        turn_values(3, picked3, v3_grouped[:])
+
+        late_codes = tile("late_codes", [P, OUTPUTS + HALF], U32, reuse="picked_scales1")
+        v_codes = late_codes[:, 0:OUTPUTS]
+        y1_codes = late_codes[:, OUTPUTS : OUTPUTS + HALF]
+        y1_scales = tile("y1_scales", [P, HALF], U8)
+        quantize(y1_codes, y1_scales[:], flat(y_grouped[1]))
+        y_codes, y_scales = (y0_codes[:], y1_codes), (y0_scales[:], y1_scales[:])
         v_scales = tile("v_scales", [P, OUTPUTS], U8)
-        for first, width, grouped in ((0, P, v0_grouped), (P, 2 * P, v12_grouped), (3 * P, P, v3_grouped)):
-            nc.vector.quantize_mx(
-                out=v_codes[:, first : first + width].bitcast(FP8X4),
-                scales=v_scales[:, first : first + width],
-                in_=grouped[:].rearrange("p e u -> p (e u)").bitcast(BF16),
-            )
+        for cols, grouped in ((slice(0, P), v0_grouped), (slice(P, 3 * P), v12_grouped), (slice(3 * P, 4 * P), v3_grouped)):
+            quantize(v_codes[:, cols], v_scales[:, cols], flat(grouped).bitcast(BF16))
 
         def finish(number, first, width, q_tiles, queue):
             cols = slice(first, first + width)
@@ -223,22 +239,22 @@ def tile_attend_mlp_reglu_topk_kernel(tc, qT, k_words, k_scales, c_words, c_scal
                 h, lo = divmod(j * P, HALF)
                 nc.tensor.matmul_mx(
                     out=acc[:, n, :],
-                    lhsT=y[h][0][:, lo : lo + P].bitcast(FP8X4),
-                    lhsT_scale=y[h][1][:, lo : lo + P],
+                    lhsT=y_codes[h][:, lo : lo + P].bitcast(FP8X4),
+                    lhsT_scale=y_scales[h][:, lo : lo + P],
                     rhs=v_codes[:, cols].bitcast(FP8X4),
                     rhs_scale=v_scales[:, cols],
                     start=True,
                     stop=True,
                 )
-            result = tile(f"result{number}", [P, len(q_tiles), width], F32)[:]
+            result = tile(f"result{number}", [P, len(q_tiles), width], F32)
             nc.vector.tensor_tensor(
-                out=result,
+                out=result[:],
                 in0=acc[:],
                 in1=bias[:, cols].unsqueeze(1).to_broadcast([P, len(q_tiles), width]),
                 op=ALU.add,
             )
             rows = out[0, q_tiles[0] * P : (q_tiles[-1] + 1) * P, cols]
-            queue.dma_start(out=rows.rearrange("(j p) e -> p j e", p=P), in_=result)
+            queue.dma_start(out=rows.rearrange("(j p) e -> p j e", p=P), in_=result[:])
 
         finish(0, 0, P, [0, 1, 2, 3], nc.sync)
         finish(1, P, 2 * P, [0, 1], nc.sync)

from contextlib import ExitStack

import concourse.mybir as mybir
from concourse.masks import make_identity

F32 = mybir.dt.float32
BF16 = mybir.dt.bfloat16
I32 = mybir.dt.int32
U32 = mybir.dt.uint32
U16 = mybir.dt.uint16
U8 = mybir.dt.uint8
FP8X4 = mybir.dt.float8_e4m3fn_x4
FP4X4 = mybir.dt.float4_e2m1fn_x4
ACT = mybir.ActivationFunctionType
ALU = mybir.AluOpType

P = 128
PACK = 4
SLOTS, NEURONS, FEATURES, QUERIES, OUTPUTS = 512, 2048, 1024, 512, 512
K_PASS = P * PACK
PASSES = FEATURES // K_PASS
TABLES = 2
SCALE_ROWS = FEATURES // 32
HALF = QUERIES // 2
LINE = 4

FLOPS = 2 * TABLES * SLOTS * FEATURES * QUERIES + 2 * SLOTS * QUERIES * OUTPUTS


def tile_attend_mlp_reglu_topk_kernel(tc, qT, k_words, k_scales, c_words, c_scales, vT, us, ob, offs, out):
    nc = tc.nc
    with ExitStack() as ctx:
        lists = ctx.enter_context(tc.tile_pool(name="lists", bufs=1))
        sbuf = ctx.enter_context(tc.tile_pool(name="sbuf", bufs=1))
        psum = ctx.enter_context(tc.psum_pool(name="psum", bufs=1))

        def tile(name, shape, dtype, reuse=None):
            return sbuf.tile(shape, dtype, name=name, tag=reuse or name, align_bytes=64)

        def bank(name, shape, number):
            return psum.tile(shape, F32, name=name, tag=f"bank{number}")

        def scalar_move(out, in_):
            nc.scalar.activation(out=out, in_=in_, func=ACT.Copy)

        def interleave(move, grouped, rows):
            move(
                out=grouped.rearrange("p (c i) t -> p c t i", i=LINE),
                in_=rows.rearrange("p t (c i) -> p c t i", i=LINE),
            )

        def quantize(codes, scales, grouped):
            nc.vector.quantize_mx(out=codes.bitcast(FP8X4), scales=scales, in_=grouped)

        def flat(grouped):
            return grouped[:].rearrange("p c t -> p (c t)")

        def load_scales(name, scales, memset):
            window = tile(name, [P, NEURONS], U8)
            memset(window[SCALE_ROWS:64, :].bitcast(I32), 0)
            memset(window[64:P, :].bitcast(I32), 0)
            nc.sync.dma_start(
                out=window[0:SCALE_ROWS, :].bitcast(I32), in_=scales.rearrange("o f n -> f o n").bitcast(I32)
            )
            return window

        def load_queries(o):
            rows = tile(f"q_rows{o}", [P, PACK, QUERIES], F32)
            features = qT[0, o * K_PASS : (o + 1) * K_PASS, :]
            nc.sync.dma_start(out=rows[:], in_=features.rearrange("(p t) q -> p t q", t=PACK))
            return rows

        def load_words(name, words, reuse=None):
            window = tile(name, [P, NEURONS], U32, reuse)
            nc.sync.dma_start(out=window[:].bitcast(I32), in_=words[0].rearrange("p n b -> p (n b)").bitcast(I32))
            return window

        def load_values(m, reuse):
            window = tile(f"v_window{m}", [P, NEURONS], F32, reuse)
            nc.sync.dma_start(out=window[:], in_=vT[m * P : (m + 1) * P, :])
            return window

        k_scale_window = load_scales("k_scale_window", k_scales, nc.vector.memset)
        offsets = lists.tile([P, SLOTS // 16], U16, name="offsets")
        nc.sync.dma_start(offsets[:], offs)
        c_scale_window = load_scales("c_scale_window", c_scales, nc.gpsimd.memset)
        q_rows0 = load_queries(0)
        k_window = load_words("k_window", k_words)
        q_rows1 = load_queries(1)

        slot_scale = tile("slot_scale", [P, PACK], F32)
        nc.scalar.dma_start(out=slot_scale[:], in_=us[0].rearrange("(p t) o -> p (t o)", t=PACK))
        bias_columns = tile("bias_columns", [P, PACK], F32)
        nc.scalar.dma_start(out=bias_columns[:], in_=ob[0].rearrange("o (p c) -> p (o c)", c=PACK))

        planes = tile("planes", [P, PASSES, TABLES, SLOTS], U8)
        nc.vector.memset(planes[:].rearrange("p o w s -> p (o w s)").bitcast(I32), 0)
        identity = tile("identity", [P, P], F32)
        make_identity(nc, identity[:])

        dealt_scales = tile("dealt_scales", [P, TABLES, SLOTS], U8)
        for w, window in enumerate((k_scale_window, c_scale_window)):
            picked_scales = tile(f"picked_scales{w}", [P, SLOTS], U8)
            nc.vector.tensor_copy(out=picked_scales[:], in_=window[:].indirect(offsets[:]))
            nc.vector.tensor_copy(
                out=dealt_scales[:, w, :].rearrange("p (t s) -> p t s", t=PACK),
                in_=picked_scales[:].rearrange("p (s t) -> p t s", t=PACK),
            )

        q_grouped0 = tile("q_grouped0", [P, QUERIES, PACK], BF16)
        interleave(scalar_move, q_grouped0[:], q_rows0[:])

        for n in range(4):
            nc.sync.dma_start(
                out=planes[32 * n : 32 * n + 4].rearrange("p o w s -> p o (w s)").bitcast(I32),
                in_=dealt_scales[8 * n : 8 * n + 8].rearrange("p w s -> p (w s)").bitcast(I32),
            )
        c_window = load_words("c_window", c_words, reuse="picked_scales1")

        def gather_words(w, window):
            picked_words = tile(f"picked_words{w}", [P, SLOTS], U32, reuse="picked_words0")
            nc.vector.tensor_copy(out=picked_words[:], in_=window[:].indirect(offsets[:]))
            halves = picked_words[:].bitcast(U16).rearrange("p (s t o) -> p o s t", t=PACK, o=PASSES)
            dealt = []
            for o in range(PASSES):
                words = tile(f"dealt_words{w}{o}", [P, SLOTS], U16)
                nc.vector.tensor_copy(out=words[:].rearrange("p (t s) -> p s t", t=PACK), in_=halves[:, o])
                dealt.append(words)
            return dealt

        q_codes, q_scales = [], []

        def score_pass(acc, w, dealt, t, o):
            cols = slice(t * P, (t + 1) * P)
            nc.tensor.matmul_mx(
                out=acc[:],
                lhsT=dealt[o][:, cols].bitcast(FP4X4),
                lhsT_scale=planes[:, o, w, cols],
                rhs=q_codes[o][:].bitcast(FP8X4),
                rhs_scale=q_scales[o][:],
                start=(o == 0),
                stop=(o == PASSES - 1),
            )

        v_windows = [load_values(0, reuse="q_rows0")]
        k_dealt = gather_words(0, k_window)
        q_codes.append(tile("q_codes0", [P, QUERIES], U32))
        q_scales.append(tile("q_scales0", [P, QUERIES], U8))
        quantize(q_codes[0][:], q_scales[0][:], flat(q_grouped0))
        v_windows.append(load_values(1, reuse="q_grouped0"))

        a = [bank(f"a{t}", [P, QUERIES], t) for t in range(PACK)]
        for t in range(PACK):
            score_pass(a[t], 0, k_dealt, t, 0)

        spread = bank("spread", [P, PACK, P], 2 * PACK - 1)
        for c in range(PACK):
            nc.tensor.transpose(spread[:, c, :], bias_columns[:, c : c + 1].to_broadcast([P, P]), identity[:])
        bias = tile("bias", [P, OUTPUTS], F32, reuse="k_window")
        scalar_move(bias[:].rearrange("x (p c) -> x p c", c=PACK), spread[:].rearrange("x c p -> x p c"))

        q1_low = tile("q1_low", [P, HALF, PACK], BF16, reuse="picked_words0")
        q1_high = tile("q1_high", [P, HALF, PACK], BF16)
        interleave(nc.vector.tensor_copy, q1_low[:], q_rows1[:, :, 0:HALF])
        interleave(scalar_move, q1_high[:], q_rows1[:, :, HALF:QUERIES])
        v_windows.append(load_values(2, reuse="q_rows1"))
        q_codes.append(tile("q_codes1", [P, QUERIES], U32))
        q_scales.append(tile("q_scales1", [P, QUERIES], U8))
        quantize(q_codes[1][:, HALF:QUERIES], q_scales[1][:, HALF:QUERIES], flat(q1_high))
        quantize(q_codes[1][:, 0:HALF], q_scales[1][:, 0:HALF], flat(q1_low))
        gates = []
        for t in range(PACK):
            score_pass(a[t], 0, k_dealt, t, 1)
            gate = tile(f"gate{t}", [P, QUERIES], F32)
            nc.scalar.activation(out=gate[:], in_=a[t][:], func=ACT.Relu)
            gates.append(gate)

        c_dealt = gather_words(1, c_window)
        v_windows.append(load_values(3, reuse="picked_scales1"))

        def gather_values(m, reuse):
            picked_values = tile(f"picked_values{m}", [P, SLOTS], BF16, reuse)
            nc.vector.tensor_copy(out=picked_values[:], in_=v_windows[m][:].indirect(offsets[:]))
            return picked_values

        def turn_values(m, picked_values, grouped):
            pairs = picked_values[:].bitcast(F32)
            turned = bank(f"turned{m}", [P, 2, P], PACK + m)
            for u in range(2):
                nc.tensor.transpose(turned[:, u, :], pairs[:, u : 2 * P : 2], identity[:])
            nc.scalar.copy(out=grouped, in_=turned[:].rearrange("p u e -> p e u"))

        picked0 = gather_values(0, reuse="q1_high")
        y_rows = tile("y_rows", [P, PACK, QUERIES], BF16, reuse="q_rows0")
        for t in range(PACK):
            z = bank(f"z{t}", [P, QUERIES], PACK + t)
            for o in range(PASSES):
                score_pass(z, 1, c_dealt, t, o)
            nc.vector.scalar_tensor_tensor(
                out=y_rows[:, t, :],
                in0=z[:],
                scalar=slot_scale[:, t : t + 1],
                in1=gates[t][:],
                op0=ALU.mult,
                op1=ALU.mult,
            )
        picked1 = gather_values(1, reuse="gate2")
        picked2 = gather_values(2, reuse="gate3")
        y_grouped = []
        for h in range(2):
            y_grouped.append(tile(f"y_grouped{h}", [P, HALF, PACK], BF16))
            interleave(nc.scalar.copy, y_grouped[h][:], y_rows[:, :, h * HALF : (h + 1) * HALF])
        y0_codes = tile("y0_codes", [P, HALF], U32)
        y0_scales = tile("y0_scales", [P, HALF], U8)
        quantize(y0_codes[:], y0_scales[:], flat(y_grouped[0]))
        v0_grouped = tile("v0_grouped", [P, P, 2], F32)
        turn_values(0, picked0, v0_grouped[:])
        picked3 = gather_values(3, reuse="y_grouped0")
        v12_grouped = tile("v12_grouped", [P, 2 * P, 2], F32, reuse="q_rows0")
        turn_values(1, picked1, v12_grouped[:, 0:P, :])
        turn_values(2, picked2, v12_grouped[:, P : 2 * P, :])
        v3_grouped = tile("v3_grouped", [P, P, 2], F32)
        turn_values(3, picked3, v3_grouped[:])

        late_codes = tile("late_codes", [P, OUTPUTS + HALF], U32, reuse="picked_scales1")
        v_codes = late_codes[:, 0:OUTPUTS]
        y1_codes = late_codes[:, OUTPUTS : OUTPUTS + HALF]
        y1_scales = tile("y1_scales", [P, HALF], U8)
        quantize(y1_codes, y1_scales[:], flat(y_grouped[1]))
        y_codes, y_scales = (y0_codes[:], y1_codes), (y0_scales[:], y1_scales[:])
        v_scales = tile("v_scales", [P, OUTPUTS], U8)
        for cols, grouped in ((slice(0, P), v0_grouped), (slice(P, 3 * P), v12_grouped), (slice(3 * P, 4 * P), v3_grouped)):
            quantize(v_codes[:, cols], v_scales[:, cols], flat(grouped).bitcast(BF16))

        def finish(number, first, width, q_tiles, queue):
            cols = slice(first, first + width)
            acc = bank(f"acc{number}", [P, len(q_tiles), width], number)
            for n, j in enumerate(q_tiles):
                h, lo = divmod(j * P, HALF)
                nc.tensor.matmul_mx(
                    out=acc[:, n, :],
                    lhsT=y_codes[h][:, lo : lo + P].bitcast(FP8X4),
                    lhsT_scale=y_scales[h][:, lo : lo + P],
                    rhs=v_codes[:, cols].bitcast(FP8X4),
                    rhs_scale=v_scales[:, cols],
                    start=True,
                    stop=True,
                )
            result = tile(f"result{number}", [P, len(q_tiles), width], F32)
            nc.vector.tensor_tensor(
                out=result[:],
                in0=acc[:],
                in1=bias[:, cols].unsqueeze(1).to_broadcast([P, len(q_tiles), width]),
                op=ALU.add,
            )
            rows = out[0, q_tiles[0] * P : (q_tiles[-1] + 1) * P, cols]
            queue.dma_start(out=rows.rearrange("(j p) e -> p j e", p=P), in_=result[:])

        finish(0, 0, P, [0, 1, 2, 3], nc.sync)
        finish(1, P, 2 * P, [0, 1], nc.sync)
        finish(2, P, 2 * P, [2, 3], nc.sync)
        finish(3, 3 * P, P, [0, 1], nc.scalar)
        finish(4, 3 * P, P, [2, 3], nc.sync)
